import numpy as np
import ml_dtypes


def mxq(x, axis, fmt="e4m3"):
    dtype, down = {"e4m3": (ml_dtypes.float8_e4m3fn, 7), "e5m2": (ml_dtypes.float8_e5m2, 14)}[fmt]
    v = np.moveaxis(np.asarray(x, np.float32).astype(ml_dtypes.bfloat16).astype(np.float64), axis, -1)
    blocks = v.reshape(v.shape[:-1] + (-1, 32))
    amax = np.abs(blocks).max(-1, keepdims=True)
    byte = np.maximum(np.where(amax > 0, np.frexp(amax)[1] - 1 + 127, 0) - down, 1)
    scale = np.exp2(byte - 127.0)
    codes = (blocks / scale).astype(np.float32).astype(dtype).astype(np.float64)
    return np.moveaxis((codes * scale).reshape(v.shape), -1, axis)


WIDE = False


def mx_kscale(k):
    if not WIDE:
        return np.ones(k)
    levels = np.array([10, -10, 5, -5, 0])
    if k % 512:
        return np.exp2(np.random.permutation(np.resize(levels, k // 32))).repeat(32)
    a = np.empty((k // 512, 16))
    for p in range(k // 512):
        a[p, :8] = np.random.permutation(np.resize(levels, 8))
        for g in range(8):
            far = levels[np.abs(levels - a[p, g]) >= 10]
            a[p, g + 8] = far[np.random.randint(len(far))]
    return np.exp2(a.ravel()).repeat(32)


def f64(x):
    return np.asarray(x).astype(np.float64)


def striped(idx):
    return np.tile(idx.reshape(-1, 16).T, (8, 1)).astype(np.uint16)


def unstriped(offs):
    return offs[:16].T.reshape(-1).astype(np.int64)


E2M1 = np.array([0.0, 0.5, 1.0, 1.5, 2.0, 3.0, 4.0, 6.0, -0.0, -0.5, -1.0, -1.5, -2.0, -3.0, -4.0, -6.0])


def pack_weight(w, fmt):
    k, n = w.shape
    w = f64(np.asarray(w, np.float32).astype(ml_dtypes.bfloat16)).reshape(k // 32, 32, n)
    amax = np.abs(w).max(1)
    if fmt == "e4m3":
        byte = np.frexp(amax)[1] - 1 + 127 - 7
    else:
        mant, ex = np.frexp(amax / 6.0)
        byte = np.where(mant > 0.5, ex, ex - 1) + 127
    byte = np.clip(np.where(amax > 0, byte, 1), 1, 254)
    scaled = (w * np.exp2(127.0 - byte)[:, None, :]).reshape(k, n).astype(np.float32)
    by_word = np.ascontiguousarray(scaled.reshape(k // 512, 128, 4, n).transpose(0, 1, 3, 2))
    if fmt == "e4m3":
        words = by_word.astype(ml_dtypes.float8_e4m3fn).view(np.uint8)
    else:
        c = by_word.astype(ml_dtypes.float4_e2m1fn).view(np.uint8) & 0xF
        words = (c[..., 0::2] | (c[..., 1::2] << 4)).reshape(k // 512, 128, 2 * n)
    return np.ascontiguousarray(words), np.ascontiguousarray(byte.astype(np.uint8).reshape(k // 512, 16, n))


def unpack_weight(words, scales, fmt):
    g, _, n = scales.shape
    words = np.ascontiguousarray(words).reshape(g, 128, n, -1)
    if fmt == "e4m3":
        vals = words.view(ml_dtypes.float8_e4m3fn).astype(np.float64)
    else:
        nib = np.empty((g, 128, n, 4), np.uint8)
        nib[..., 0::2] = words & 0xF
        nib[..., 1::2] = words >> 4
        vals = E2M1[nib]
    vals = vals * np.repeat(np.exp2(scales.astype(np.float64) - 127.0), 8, axis=1)[..., None]
    return vals.transpose(0, 1, 3, 2).reshape(g * 512, n)


def gelu(v):
    return 0.5 * v * (1.0 + np.tanh(np.sqrt(2.0 / np.pi) * (v + 0.044715 * v**3)))


K, T, S, S2 = 1024, 4096, 1024, 512


def setup_inputs():
    n = np.random.standard_normal
    s = mx_kscale(K)[:, None]
    d = {}
    d["tab_words"], d["tab_scales"] = pack_weight(n((K, T)) * s, "e4m3")
    d["offs"] = striped(np.random.permutation(T)[:S])
    d["offs2"] = striped(np.random.permutation(T)[:S2])
    d["w1"] = (1.5 * n((K, K)) / K ** 0.5 / s).astype(np.float32)
    d["w4_words"], d["w4_scales"] = pack_weight(n((K, K)) / K ** 0.5 / s, "e2m1")
    d["ga"] = (1.3 * np.exp(0.3 * n(K)) / K ** 0.5 / s[:, 0]).astype(np.float32)
    d["gb"] = (0.9 * np.exp(0.3 * n(K)) / K ** 0.5 / s[:, 0]).astype(np.float32)
    d["th"] = (0.8 * n(S2)).astype(np.float32)
    return d


def reference(tab_words, tab_scales, offs, offs2, w1, w4_words, w4_scales, ga, gb, th):
    TW = unpack_weight(tab_words, tab_scales, "e4m3")
    v = TW[:, unstriped(offs)]
    v2 = TW[:, unstriped(offs2)]
    w4 = unpack_weight(w4_words, w4_scales, "e2m1")
    b = mxq(f64(w1), 0, "e4m3").T @ v
    l = w4.T @ v
    h = f64(ga)[:, None] * np.tanh(b) + f64(gb)[:, None] * l
    e = v2.T @ mxq(h, 0, "e4m3")
    y = e - f64(th)[:, None]
    return y / (1.0 + np.exp(-y))

@@ -1,0 +1,311 @@
+from contextlib import ExitStack
+
+import concourse.mybir as mybir
+
+K, T, S, S2 = 1024, 4096, 1024, 512
+FLOPS = 2 * K * K * S * 2 + 2 * K * S2 * S
+
+F32 = mybir.dt.float32
+BF16 = mybir.dt.bfloat16
+I32 = mybir.dt.int32
+U32 = mybir.dt.uint32
+U16 = mybir.dt.uint16
+U8 = mybir.dt.uint8
+FP8X4 = mybir.dt.float8_e4m3fn_x4
+FP4X4 = mybir.dt.float4_e2m1fn_x4
+ACT = mybir.ActivationFunctionType
+ALU = mybir.AluOpType
+
+P = 128
+PACK = 4
+PASSES = K // (P * PACK)
+N = 512
+HALVES = S // N
+QUADS = 4
+M_TILES = S2 // P
+
+
+def tile_list_track_blend_rating_kernel(
+    tc, tab_words, tab_scales, offs, offs2, w1, w4_words, w4_scales, ga, gb, th, out
+):
+    nc = tc.nc
+    with ExitStack() as ctx:
+        keep = ctx.enter_context(tc.tile_pool(name="keep", bufs=1))
+        shared = ctx.enter_context(tc.tile_pool(name="shared", bufs=1))
+        ring = ctx.enter_context(tc.tile_pool(name="ring", bufs=2))
+        psum = ctx.enter_context(tc.psum_pool(name="psum", bufs=8))
+
+        def held(shape, dtype, name):
+            return keep.tile(shape, dtype, name=name, align_bytes=64)
+
+        idx = held([P, S // 16], U16, "idx")
+        idx2 = held([P, S2 // 16], U16, "idx2")
+        chunk_bytes = PACK * N * 4
+        tab_s = shared.tile([P, T], U8, name="tab_s", align_bytes=64, offset=chunk_bytes - T // 2)
+        w4_s_raw = shared.tile([P, PASSES * K], U8, name="w4_s_raw", align_bytes=64, offset=3 * chunk_bytes - K)
+        v_s1 = held([P, S], U8, "v_s1")
+        zero_in = held([P, 1], F32, "zero_in")
+        zero = held([P, 1], F32, "zero")
+
+        split = 640
+        nc.gpsimd.memset(tab_s[:].bitcast(I32)[:, :split], 0)
+        nc.vector.memset(tab_s[:].bitcast(I32)[:, split:], 0)
+        nc.vector.memset(w4_s_raw[:].bitcast(I32), 0)
+        nc.vector.memset(zero_in[:], 0.0)
+        nc.vector.memset(v_s1[:].bitcast(I32), 0)
+        nc.scalar.activation(zero[:], zero_in[:], ACT.Silu)
+
+        nc.sync.dma_start(idx[:], offs)
+        nc.sync.dma_start(idx2[:], offs2)
+        w4_raw = held([P, PASSES, K // 2], I32, "w4_raw")
+        nc.sync.dma_start(w4_raw[:], w4_words.bitcast(I32).rearrange("a p c -> p a c"))
+        tab_w = [held([P, T], I32, f"tab_w{a}") for a in range(PASSES)]
+        tab_src = [tab_words[a].rearrange("p t i -> p (t i)").bitcast(I32) for a in range(PASSES)]
+        for q in range(QUADS):
+            nc.sync.dma_start(
+                tab_s[32 * q : 32 * q + 4 * PASSES, :].bitcast(I32),
+                tab_scales[:, 4 * q : 4 * q + 4, :].bitcast(I32),
+            )
+        nc.sync.dma_start(tab_w[0][:, : T // 2], tab_src[0][:, : T // 2])
+        for q in range(QUADS):
+            nc.sync.dma_start(
+                w4_s_raw[32 * q : 32 * q + 4, :].bitcast(I32).rearrange("r (a c) -> r a c", a=PASSES),
+                w4_scales[:, 4 * q : 4 * q + 4, :].bitcast(I32).rearrange("a r c -> r a c"),
+            )
+        nc.sync.dma_start(tab_w[0][:, T // 2 :], tab_src[0][:, T // 2 :])
+        nc.sync.dma_start(tab_w[1][:], tab_src[1])
+        ga_t = held([P, PASSES, PACK], F32, "ga_t")
+        gb_t = held([P, PASSES, PACK], F32, "gb_t")
+        th_t = held([P, M_TILES], F32, "th_t")
+        neg_th = held([P, M_TILES], F32, "neg_th")
+        nc.sync.dma_start(gb_t[:], gb.rearrange("(b p t) -> p b t", b=PASSES, t=PACK))
+        nc.sync.dma_start(ga_t[:], ga.rearrange("(b p t) -> p b t", b=PASSES, t=PACK))
+        with nc.allow_non_contiguous_dma(reason="one threshold a partition"):
+            nc.sync.dma_start(th_t[:], th.rearrange("(u p) -> p u", p=P))
+        nc.scalar.mul(neg_th[:], th_t[:], -1.0)
+
+        w4_w = held([P, PASSES * K], U16, "w4_w")
+        nc.vector.tensor_copy(
+            w4_w[:].rearrange("p (g t m) -> p g t m", t=PACK, m=P),
+            w4_raw[:].rearrange("p a c -> p (a c)").bitcast(U16).rearrange("p (g m t) -> p g t m", t=PACK, m=P),
+        )
+
+        v_s = held([P, S], U8, "v_s")
+        nc.vector.tensor_copy(v_s[:], tab_s[:].indirect(idx[:]))
+        nc.sync.dma_start(v_s1[0:100, :].bitcast(I32), v_s[4:104, :].bitcast(I32))
+        v2_s = held([P, S2], U8, "v2_s")
+        nc.vector.tensor_copy(v2_s[:], tab_s[:].indirect(idx2[:]))
+        w4_s = held([P, PASSES * K], U8, "w4_s")
+        nc.vector.tensor_copy(
+            w4_s[:].rearrange("p (g t m) -> p g t m", t=PACK, m=P),
+            w4_s_raw[:].rearrange("p (g m t) -> p g t m", t=PACK, m=P),
+        )
+        w1_raw = {}
+        for rb in range(PASSES):
+            for a in range(PASSES):
+                raw = shared.tile(
+                    [P, PACK, N], F32, name=f"w1_raw{rb}{a}", align_bytes=64, offset=(rb * PASSES + a) * chunk_bytes
+                )
+                nc.sync.dma_start(
+                    raw[:],
+                    w1[512 * a : 512 * (a + 1), N * rb : N * (rb + 1)].rearrange("(p i) c -> p i c", i=PACK),
+                )
+                w1_raw[rb, a] = raw
+        v_w = {}
+        v2_w = {}
+
+        def gather_v(a):
+            for jh in range(HALVES):
+                words = held([P, N], U32, f"v_w{a}{jh}")
+                cols = slice(jh * N // 16, (jh + 1) * N // 16)
+                nc.vector.tensor_copy(words[:], tab_w[a][:].bitcast(U32).indirect(idx[:, cols]))
+                v_w[a, jh] = words
+
+        def gather_v2(a):
+            words = held([P, S2], U32, f"v2_w{a}")
+            nc.vector.tensor_copy(words[:], tab_w[a][:].bitcast(U32).indirect(idx2[:]))
+            v2_w[a] = words
+
+        gather_v(0)
+        gather_v(1)
+
+        def bank(name):
+            return psum.tile([P, N], F32, name=name, tag="bank")
+
+        lin = {}
+
+        def l_pass(acc, rb, jh, t, a):
+            c0 = a * K + rb * N + t * P
+            planes = v_s if a == 0 else v_s1
+            nc.tensor.matmul_mx(
+                out=acc[:],
+                lhsT=w4_w[:, c0 : c0 + P].bitcast(U8).bitcast(FP4X4),
+                lhsT_scale=w4_s[:, c0 : c0 + P],
+                rhs=v_w[a, jh][:].bitcast(FP8X4),
+                rhs_scale=planes[:, jh * N : (jh + 1) * N],
+                start=(a == 0),
+                stop=(a == PASSES - 1),
+            )
+
+        def l_out(acc, rb, jh, t):
+            scaled = held([P, N], F32, f"lin{rb}{jh}{t}")
+            nc.scalar.activation(scaled[:], acc[:], ACT.Copy, scale=gb_t[:, rb, t : t + 1])
+            lin[rb, jh, t] = scaled
+
+        def l_groups(groups):
+            tiles = [(rb, jh, t) for rb, jh in groups for t in range(PACK)]
+            accs = {key: bank(f"l{key[0]}{key[1]}{key[2]}") for key in tiles}
+            for a in range(PASSES):
+                for key in tiles:
+                    l_pass(accs[key], *key, a)
+            for key in tiles:
+                l_out(accs[key], *key)
+
+        w1_bf = {}
+        w1_w = {}
+        w1_s = {}
+
+        def w1_cast(rb, a, tp, on_scalar):
+            grouped = held([P, 2, P, PACK], BF16, f"w1_bf{rb}{a}{tp}")
+            src = w1_raw[rb, a][:].rearrange("p i (m t) -> p m i t", t=PACK)[:, :, :, 2 * tp : 2 * tp + 2]
+            dst = grouped[:].rearrange("p t m i -> p m i t")
+            if on_scalar:
+                nc.scalar.copy(dst, src)
+            else:
+                nc.vector.tensor_copy(dst, src)
+            w1_bf[rb, a, tp] = grouped
+
+        def w1_quant(rb, a, tp):
+            codes = held([P, 2 * P], U32, f"w1_w{rb}{a}{tp}")
+            scales = held([P, 2 * P], U8, f"w1_s{rb}{a}{tp}")
+            nc.vector.quantize_mx(
+                out=codes[:].bitcast(FP8X4),
+                scales=scales[:],
+                in_=w1_bf[rb, a, tp][:].rearrange("p t m i -> p (t m i)"),
+            )
+            w1_w[rb, a, tp] = codes
+            w1_s[rb, a, tp] = scales
+
+        def w1_chunk(rb, a, scalar_pairs):
+            for tp in range(2):
+                w1_cast(rb, a, tp, tp in scalar_pairs)
+            for tp in range(2):
+                w1_quant(rb, a, tp)
+
+        h_w = {}
+        h_s = {}
+        bounded = {}
+        rows = {}
+
+        def b_tile(rb, j0, width, t):
+            jh, c0 = divmod(j0, N)
+            acc = bank(f"b{rb}{j0}{t}")
+            cols = slice((t % 2) * P, (t % 2 + 1) * P)
+            for a in range(PASSES):
+                nc.tensor.matmul_mx(
+                    out=acc[:, :width],
+                    lhsT=w1_w[rb, a, t // 2][:, cols].bitcast(FP8X4),
+                    lhsT_scale=w1_s[rb, a, t // 2][:, cols],
+                    rhs=v_w[a, jh][:, c0 : c0 + width].bitcast(FP8X4),
+                    rhs_scale=v_s[4 * a : P, j0 : j0 + width],
+                    start=(a == 0),
+                    stop=(a == PASSES - 1),
+                )
+            values = ring.tile([P, width], F32, name="bounded", bufs=8, align_bytes=64)
+            nc.scalar.activation(values[:], acc[:, :width], ACT.Tanh, bias=zero[:])
+            bounded[rb, j0, t] = values
+
+        def h_row(rb, j0, width, t):
+            jh, c0 = divmod(j0, N)
+            if t == 0:
+                rows[rb, j0] = ring.tile([P, PACK, width], BF16, name="h_rows", align_bytes=64)
+            nc.vector.scalar_tensor_tensor(
+                out=rows[rb, j0][:, t, :],
+                in0=bounded[rb, j0, t][:],
+                scalar=ga_t[:, rb, t : t + 1],
+                in1=lin[rb, jh, t][:, c0 : c0 + width],
+                op0=ALU.mult,
+                op1=ALU.add,
+            )
+
+        woven = {}
+
+        def h_weave(rb, j0, width, copy=nc.vector.tensor_copy):
+            woven[rb, j0] = ring.tile([P, width, PACK], BF16, name="h_woven", align_bytes=64)
+            copy(
+                woven[rb, j0][:].rearrange("p (c i) t -> p c t i", i=4),
+                rows[rb, j0][:].rearrange("p t (c i) -> p c t i", i=4),
+            )
+
+        def h_quant(rb, j0, width):
+            codes = held([P, width], U32, f"h_w{rb}{j0}")
+            scales = held([P, width], U8, f"h_s{rb}{j0}")
+            nc.vector.quantize_mx(
+                out=codes[:].bitcast(FP8X4), scales=scales[:], in_=woven[rb, j0][:].rearrange("p n t -> p (n t)")
+            )
+            h_w[rb, j0] = codes
+            h_s[rb, j0] = scales
+
+        def h_cols(planes, rb, j0, width):
+            start = max(s for r, s in planes if r == rb and s <= j0)
+            return planes[rb, start][:, j0 - start : j0 - start + width]
+
+        def rate(j0, width):
+            for u in range(M_TILES):
+                acc = bank(f"e{j0}{u}")
+                cols = slice(u * P, (u + 1) * P)
+                for rb in range(PASSES):
+                    nc.tensor.matmul_mx(
+                        out=acc[:, :width],
+                        lhsT=v2_w[rb][:, cols].bitcast(FP8X4),
+                        lhsT_scale=v2_s[4 * rb : P, cols],
+                        rhs=h_cols(h_w, rb, j0, width).bitcast(FP8X4),
+                        rhs_scale=h_cols(h_s, rb, j0, width),
+                        start=(rb == 0),
+                        stop=(rb == PASSES - 1),
+                    )
+                result = ring.tile([P, width], F32, name="result", bufs=12, align_bytes=64)
+                nc.scalar.activation(result[:], acc[:, :width], ACT.Silu, bias=neg_th[:, u : u + 1])
+                nc.sync.dma_start(out[u * P : (u + 1) * P, j0 : j0 + width], result[:])
+
+        def b_group(rb, j0, width):
+            for t in range(PACK):
+                b_tile(rb, j0, width, t)
+
+        def h_rows(rb, j0, width):
+            for t in range(PACK):
+                h_row(rb, j0, width, t)
+
+        l_groups([(0, 0), (0, 1)])
+        l_groups([(1, 0)])
+        w1_chunk(0, 0, ())
+        w1_chunk(0, 1, ())
+        l_groups([(1, 1)])
+        b_group(0, 0, N)
+        w1_chunk(1, 0, ())
+        b_group(0, N, N)
+        h_rows(0, 0, N)
+        w1_chunk(1, 1, ())
+        h_weave(0, 0, N)
+        b_group(1, 0, N)
+        h_rows(0, N, N)
+        h_quant(0, 0, N)
+        half = N // 2
+        b_group(1, N, half)
+        b_group(1, N + half, half)
+        h_weave(0, N, N, nc.scalar.copy)
+        h_rows(1, 0, N)
+        h_weave(1, 0, N)
+        gather_v2(0)
+        gather_v2(1)
+        h_quant(1, 0, N)
+        rate(0, N)
+        h_rows(1, N, half)
+        h_quant(0, N, N)
+        h_weave(1, N, half)
+        h_rows(1, N + half, half)
+        h_quant(1, N, half)
+        h_weave(1, N + half, half)
+        rate(N, half)
+        h_quant(1, N + half, half)
+        rate(N + half, half)

@@ -41,9 +41,15 @@ def tile_list_track_blend_rating_kernel(
         idx = held([P, S // 16], U16, "idx")
         idx2 = held([P, S2 // 16], U16, "idx2")
         chunk_bytes = PACK * N * 4
-        tab_s = shared.tile([P, T], U8, name="tab_s", align_bytes=64, offset=chunk_bytes - T // 2)
-        w4_s_raw = shared.tile([P, PASSES * K], U8, name="w4_s_raw", align_bytes=64, offset=3 * chunk_bytes - K)
-        v_s1 = held([P, S], U8, "v_s1")
+        small = 64
+        chunk_at = [0, chunk_bytes + 2 * small, 2 * chunk_bytes + 2 * small, 3 * chunk_bytes + 3 * small]
+
+        def placed(shape, dtype, name, offset):
+            return shared.tile(shape, dtype, name=name, align_bytes=64, offset=offset)
+
+        tab_s = placed([P, T], U8, "tab_s", chunk_at[1] - T // 2)
+        w4_s_raw = placed([P, PASSES * K], U8, "w4_s_raw", chunk_at[3] - K)
+        plane1 = held([P, S + S2], U8, "plane1")
         zero_in = held([P, 1], F32, "zero_in")
         zero = held([P, 1], F32, "zero")
 
@@ -52,7 +58,7 @@ def tile_list_track_blend_rating_kernel(
         nc.vector.memset(tab_s[:].bitcast(I32)[:, split:], 0)
         nc.vector.memset(w4_s_raw[:].bitcast(I32), 0)
         nc.vector.memset(zero_in[:], 0.0)
-        nc.vector.memset(v_s1[:].bitcast(I32), 0)
+        nc.vector.memset(plane1[:].bitcast(I32), 0)
         nc.scalar.activation(zero[:], zero_in[:], ACT.Silu)
 
         nc.sync.dma_start(idx[:], offs)
@@ -63,9 +69,10 @@ def tile_list_track_blend_rating_kernel(
         tab_src = [tab_words[a].rearrange("p t i -> p (t i)").bitcast(I32) for a in range(PASSES)]
         for q in range(QUADS):
             nc.sync.dma_start(
-                tab_s[32 * q : 32 * q + 4 * PASSES, :].bitcast(I32),
-                tab_scales[:, 4 * q : 4 * q + 4, :].bitcast(I32),
+                tab_s[32 * q : 32 * q + 4, :].bitcast(I32),
+                tab_scales[0, 4 * q : 4 * q + 4, :].bitcast(I32),
             )
+        nc.sync.dma_start(tab_s[4:P:8, :].bitcast(I32), tab_scales[1].bitcast(I32))
         nc.sync.dma_start(tab_w[0][:, : T // 2], tab_src[0][:, : T // 2])
         for q in range(QUADS):
             nc.sync.dma_start(
@@ -74,15 +81,6 @@ def tile_list_track_blend_rating_kernel(
             )
         nc.sync.dma_start(tab_w[0][:, T // 2 :], tab_src[0][:, T // 2 :])
         nc.sync.dma_start(tab_w[1][:], tab_src[1])
-        ga_t = held([P, PASSES, PACK], F32, "ga_t")
-        gb_t = held([P, PASSES, PACK], F32, "gb_t")
-        th_t = held([P, M_TILES], F32, "th_t")
-        neg_th = held([P, M_TILES], F32, "neg_th")
-        nc.sync.dma_start(gb_t[:], gb.rearrange("(b p t) -> p b t", b=PASSES, t=PACK))
-        nc.sync.dma_start(ga_t[:], ga.rearrange("(b p t) -> p b t", b=PASSES, t=PACK))
-        with nc.allow_non_contiguous_dma(reason="one threshold a partition"):
-            nc.sync.dma_start(th_t[:], th.rearrange("(u p) -> p u", p=P))
-        nc.scalar.mul(neg_th[:], th_t[:], -1.0)
 
         w4_w = held([P, PASSES * K], U16, "w4_w")
         nc.vector.tensor_copy(
@@ -90,27 +88,42 @@ def tile_list_track_blend_rating_kernel(
             w4_raw[:].rearrange("p a c -> p (a c)").bitcast(U16).rearrange("p (g m t) -> p g t m", t=PACK, m=P),
         )
 
-        v_s = held([P, S], U8, "v_s")
-        nc.vector.tensor_copy(v_s[:], tab_s[:].indirect(idx[:]))
-        nc.sync.dma_start(v_s1[0:100, :].bitcast(I32), v_s[4:104, :].bitcast(I32))
-        v2_s = held([P, S2], U8, "v2_s")
-        nc.vector.tensor_copy(v2_s[:], tab_s[:].indirect(idx2[:]))
+        plane0 = held([P, S + S2], U8, "plane0")
+        nc.vector.tensor_copy(plane0[:, :S], tab_s[:].indirect(idx[:]))
+        nc.vector.tensor_copy(plane0[:, S:], tab_s[:].indirect(idx2[:]))
+        for q in range(QUADS):
+            nc.sync.dma_start(
+                plane1[32 * q : 32 * q + 4, :].bitcast(I32),
+                plane0[32 * q + 4 : 32 * q + 32 : 8, :].bitcast(I32),
+            )
+        planes = (plane0, plane1)
         w4_s = held([P, PASSES * K], U8, "w4_s")
         nc.vector.tensor_copy(
             w4_s[:].rearrange("p (g t m) -> p g t m", t=PACK, m=P),
             w4_s_raw[:].rearrange("p (g m t) -> p g t m", t=PACK, m=P),
         )
+        gb_t = placed([P, PASSES, PACK], F32, "gb_t", chunk_at[1] - 2 * small)
+        ga_t = placed([P, PASSES, PACK], F32, "ga_t", chunk_at[1] - small)
+        th_t = placed([P, M_TILES], F32, "th_t", chunk_at[3] - small)
+        neg_th = held([P, M_TILES], F32, "neg_th")
         w1_raw = {}
-        for rb in range(PASSES):
-            for a in range(PASSES):
-                raw = shared.tile(
-                    [P, PACK, N], F32, name=f"w1_raw{rb}{a}", align_bytes=64, offset=(rb * PASSES + a) * chunk_bytes
-                )
-                nc.sync.dma_start(
-                    raw[:],
-                    w1[512 * a : 512 * (a + 1), N * rb : N * (rb + 1)].rearrange("(p i) c -> p i c", i=PACK),
-                )
-                w1_raw[rb, a] = raw
+
+        def load_w1(rb, a):
+            raw = placed([P, PACK, N], F32, f"w1_raw{rb}{a}", chunk_at[rb * PASSES + a])
+            nc.sync.dma_start(
+                raw[:],
+                w1[512 * a : 512 * (a + 1), N * rb : N * (rb + 1)].rearrange("(p i) c -> p i c", i=PACK),
+            )
+            w1_raw[rb, a] = raw
+
+        nc.sync.dma_start(gb_t[:], gb.rearrange("(b p t) -> p b t", b=PASSES, t=PACK))
+        load_w1(0, 0)
+        load_w1(0, 1)
+        nc.sync.dma_start(ga_t[:], ga.rearrange("(b p t) -> p b t", b=PASSES, t=PACK))
+        load_w1(1, 0)
+        load_w1(1, 1)
+        with nc.allow_non_contiguous_dma(reason="one threshold a partition"):
+            nc.sync.dma_start(th_t[:], th.rearrange("(u p) -> p u", p=P))
         v_w = {}
         v2_w = {}
 
@@ -136,13 +149,12 @@ def tile_list_track_blend_rating_kernel(
 
         def l_pass(acc, rb, jh, t, a):
             c0 = a * K + rb * N + t * P
-            planes = v_s if a == 0 else v_s1
             nc.tensor.matmul_mx(
                 out=acc[:],
                 lhsT=w4_w[:, c0 : c0 + P].bitcast(U8).bitcast(FP4X4),
                 lhsT_scale=w4_s[:, c0 : c0 + P],
                 rhs=v_w[a, jh][:].bitcast(FP8X4),
-                rhs_scale=planes[:, jh * N : (jh + 1) * N],
+                rhs_scale=planes[a][:, jh * N : (jh + 1) * N],
                 start=(a == 0),
                 stop=(a == PASSES - 1),
             )
@@ -207,7 +219,7 @@ def tile_list_track_blend_rating_kernel(
                     lhsT=w1_w[rb, a, t // 2][:, cols].bitcast(FP8X4),
                     lhsT_scale=w1_s[rb, a, t // 2][:, cols],
                     rhs=v_w[a, jh][:, c0 : c0 + width].bitcast(FP8X4),
-                    rhs_scale=v_s[4 * a : P, j0 : j0 + width],
+                    rhs_scale=planes[a][:, j0 : j0 + width],
                     start=(a == 0),
                     stop=(a == PASSES - 1),
                 )
@@ -218,7 +230,7 @@ def tile_list_track_blend_rating_kernel(
         def h_row(rb, j0, width, t):
             jh, c0 = divmod(j0, N)
             if t == 0:
-                rows[rb, j0] = ring.tile([P, PACK, width], BF16, name="h_rows", align_bytes=64)
+                rows[rb, j0] = ring.tile([P, PACK, width], BF16, name="h_rows", bufs=3, align_bytes=64)
             nc.vector.scalar_tensor_tensor(
                 out=rows[rb, j0][:, t, :],
                 in0=bounded[rb, j0, t][:],
@@ -231,7 +243,7 @@ def tile_list_track_blend_rating_kernel(
         woven = {}
 
         def h_weave(rb, j0, width, copy=nc.vector.tensor_copy):
-            woven[rb, j0] = ring.tile([P, width, PACK], BF16, name="h_woven", align_bytes=64)
+            woven[rb, j0] = ring.tile([P, width, PACK], BF16, name="h_woven", bufs=3, align_bytes=64)
             copy(
                 woven[rb, j0][:].rearrange("p (c i) t -> p c t i", i=4),
                 rows[rb, j0][:].rearrange("p t (c i) -> p c t i", i=4),
@@ -246,9 +258,12 @@ def tile_list_track_blend_rating_kernel(
             h_w[rb, j0] = codes
             h_s[rb, j0] = scales
 
-        def h_cols(planes, rb, j0, width):
-            start = max(s for r, s in planes if r == rb and s <= j0)
-            return planes[rb, start][:, j0 - start : j0 - start + width]
+        def h_cols(pieces, rb, j0, width):
+            start = max(s for r, s in pieces if r == rb and s <= j0)
+            return pieces[rb, start][:, j0 - start : j0 - start + width]
+
+        def negate_th():
+            nc.scalar.mul(neg_th[:], th_t[:], -1.0)
 
         def rate(j0, width):
             for u in range(M_TILES):
@@ -258,7 +273,7 @@ def tile_list_track_blend_rating_kernel(
                     nc.tensor.matmul_mx(
                         out=acc[:, :width],
                         lhsT=v2_w[rb][:, cols].bitcast(FP8X4),
-                        lhsT_scale=v2_s[4 * rb : P, cols],
+                        lhsT_scale=planes[rb][:, S + u * P : S + (u + 1) * P],
                         rhs=h_cols(h_w, rb, j0, width).bitcast(FP8X4),
                         rhs_scale=h_cols(h_s, rb, j0, width),
                         start=(rb == 0),
@@ -276,36 +291,40 @@ def tile_list_track_blend_rating_kernel(
             for t in range(PACK):
                 h_row(rb, j0, width, t)
 
-        l_groups([(0, 0), (0, 1)])
-        l_groups([(1, 0)])
-        w1_chunk(0, 0, ())
-        w1_chunk(0, 1, ())
-        l_groups([(1, 1)])
-        b_group(0, 0, N)
-        w1_chunk(1, 0, ())
-        b_group(0, N, N)
-        h_rows(0, 0, N)
-        w1_chunk(1, 1, ())
-        h_weave(0, 0, N)
-        b_group(1, 0, N)
-        h_rows(0, N, N)
-        h_quant(0, 0, N)
-        half = N // 2
-        b_group(1, N, half)
-        b_group(1, N + half, half)
-        h_weave(0, N, N, nc.scalar.copy)
-        h_rows(1, 0, N)
-        h_weave(1, 0, N)
+        l_groups([(0, 0), (1, 0)])
         gather_v2(0)
         gather_v2(1)
-        h_quant(1, 0, N)
-        rate(0, N)
-        h_rows(1, N, half)
-        h_quant(0, N, N)
-        h_weave(1, N, half)
-        h_rows(1, N + half, half)
-        h_quant(1, N, half)
-        h_weave(1, N + half, half)
-        rate(N, half)
-        h_quant(1, N + half, half)
-        rate(N + half, half)
+        w1_chunk(0, 0, ())
+        l_groups([(0, 1)])
+        w1_chunk(0, 1, ())
+        b_group(0, 0, N)
+        w1_chunk(1, 0, ())
+        l_groups([(1, 1)])
+        w1_chunk(1, 1, ())
+        negate_th()
+        b_group(1, 0, 512)
+        h_rows(0, 0, 512)
+        b_group(0, 512, 256)
+        h_weave(0, 0, 512, nc.scalar.copy)
+        h_rows(1, 0, 512)
+        b_group(1, 512, 256)
+        h_quant(0, 0, 512)
+        h_weave(1, 0, 512)
+        h_rows(0, 512, 256)
+        b_group(0, 768, 256)
+        h_quant(1, 0, 512)
+        rate(0, 512)
+        h_weave(0, 512, 256)
+        h_rows(1, 512, 256)
+        b_group(1, 768, 256)
+        h_quant(0, 512, 256)
+        h_weave(1, 512, 256)
+        h_rows(0, 768, 256)
+        h_quant(1, 512, 256)
+        rate(512, 256)
+        h_weave(0, 768, 256)
+        h_rows(1, 768, 256)
+        h_quant(0, 768, 256)
+        h_weave(1, 768, 256)
+        h_quant(1, 768, 256)
+        rate(768, 256)

@@ -42,7 +42,7 @@ def tile_list_track_blend_rating_kernel(
         idx2 = held([P, S2 // 16], U16, "idx2")
         chunk_bytes = PACK * N * 4
         small = 64
-        chunk_at = [0, chunk_bytes + 2 * small, 2 * chunk_bytes + 2 * small, 3 * chunk_bytes + 3 * small]
+        chunk_at = [0, chunk_bytes + small, 2 * chunk_bytes + small, 3 * chunk_bytes + 3 * small]
 
         def placed(shape, dtype, name, offset):
             return shared.tile(shape, dtype, name=name, align_bytes=64, offset=offset)
@@ -67,17 +67,14 @@ def tile_list_track_blend_rating_kernel(
         nc.sync.dma_start(w4_raw[:], w4_words.bitcast(I32).rearrange("a p c -> p a c"))
         tab_w = [held([P, T], I32, f"tab_w{a}") for a in range(PASSES)]
         tab_src = [tab_words[a].rearrange("p t i -> p (t i)").bitcast(I32) for a in range(PASSES)]
-        for q in range(QUADS):
-            nc.sync.dma_start(
-                tab_s[32 * q : 32 * q + 4, :].bitcast(I32),
-                tab_scales[0, 4 * q : 4 * q + 4, :].bitcast(I32),
-            )
+        for r in range(4):
+            nc.sync.dma_start(tab_s[r:P:32, :].bitcast(I32), tab_scales[0, r:16:4, :].bitcast(I32))
         nc.sync.dma_start(tab_s[4:P:8, :].bitcast(I32), tab_scales[1].bitcast(I32))
         nc.sync.dma_start(tab_w[0][:, : T // 2], tab_src[0][:, : T // 2])
-        for q in range(QUADS):
+        for r in range(4):
             nc.sync.dma_start(
-                w4_s_raw[32 * q : 32 * q + 4, :].bitcast(I32).rearrange("r (a c) -> r a c", a=PASSES),
-                w4_scales[:, 4 * q : 4 * q + 4, :].bitcast(I32).rearrange("a r c -> r a c"),
+                w4_s_raw[r:P:32, :].bitcast(I32).rearrange("q (a c) -> q a c", a=PASSES),
+                w4_scales[:, r:16:4, :].bitcast(I32).rearrange("a q c -> q a c"),
             )
         nc.sync.dma_start(tab_w[0][:, T // 2 :], tab_src[0][:, T // 2 :])
         nc.sync.dma_start(tab_w[1][:], tab_src[1])
@@ -91,19 +88,16 @@ def tile_list_track_blend_rating_kernel(
         plane0 = held([P, S + S2], U8, "plane0")
         nc.vector.tensor_copy(plane0[:, :S], tab_s[:].indirect(idx[:]))
         nc.vector.tensor_copy(plane0[:, S:], tab_s[:].indirect(idx2[:]))
-        for q in range(QUADS):
-            nc.sync.dma_start(
-                plane1[32 * q : 32 * q + 4, :].bitcast(I32),
-                plane0[32 * q + 4 : 32 * q + 32 : 8, :].bitcast(I32),
-            )
+        for r in range(4):
+            nc.sync.dma_start(plane1[r:P:32, :].bitcast(I32), plane0[4 + 8 * r : P : 32, :].bitcast(I32))
         planes = (plane0, plane1)
         w4_s = held([P, PASSES * K], U8, "w4_s")
         nc.vector.tensor_copy(
             w4_s[:].rearrange("p (g t m) -> p g t m", t=PACK, m=P),
             w4_s_raw[:].rearrange("p (g m t) -> p g t m", t=PACK, m=P),
         )
-        gb_t = placed([P, PASSES, PACK], F32, "gb_t", chunk_at[1] - 2 * small)
-        ga_t = placed([P, PASSES, PACK], F32, "ga_t", chunk_at[1] - small)
+        gb_t = placed([P, PASSES, PACK], F32, "gb_t", chunk_at[1] - small)
+        ga_t = placed([P, PASSES, PACK], F32, "ga_t", chunk_at[3] - 2 * small)
         th_t = placed([P, M_TILES], F32, "th_t", chunk_at[3] - small)
         neg_th = held([P, M_TILES], F32, "neg_th")
         w1_raw = {}
@@ -119,8 +113,8 @@ def tile_list_track_blend_rating_kernel(
         nc.sync.dma_start(gb_t[:], gb.rearrange("(b p t) -> p b t", b=PASSES, t=PACK))
         load_w1(0, 0)
         load_w1(0, 1)
-        nc.sync.dma_start(ga_t[:], ga.rearrange("(b p t) -> p b t", b=PASSES, t=PACK))
         load_w1(1, 0)
+        nc.sync.dma_start(ga_t[:], ga.rearrange("(b p t) -> p b t", b=PASSES, t=PACK))
         load_w1(1, 1)
         with nc.allow_non_contiguous_dma(reason="one threshold a partition"):
             nc.sync.dma_start(th_t[:], th.rearrange("(u p) -> p u", p=P))
@@ -303,26 +297,26 @@ def tile_list_track_blend_rating_kernel(
         w1_chunk(1, 1, ())
         negate_th()
         b_group(1, 0, 512)
-        h_rows(0, 0, 512)
         b_group(0, 512, 256)
+        h_rows(0, 0, 512)
+        b_group(1, 512, 256)
         h_weave(0, 0, 512, nc.scalar.copy)
         h_rows(1, 0, 512)
-        b_group(1, 512, 256)
+        b_group(0, 768, 256)
         h_quant(0, 0, 512)
         h_weave(1, 0, 512)
         h_rows(0, 512, 256)
-        b_group(0, 768, 256)
+        b_group(1, 768, 256)
         h_quant(1, 0, 512)
         rate(0, 512)
         h_weave(0, 512, 256)
         h_rows(1, 512, 256)
-        b_group(1, 768, 256)
         h_quant(0, 512, 256)
         h_weave(1, 512, 256)
         h_rows(0, 768, 256)
+        h_weave(0, 768, 256, nc.scalar.copy)
         h_quant(1, 512, 256)
         rate(512, 256)
-        h_weave(0, 768, 256)
         h_rows(1, 768, 256)
         h_quant(0, 768, 256)
         h_weave(1, 768, 256)

@@ -18,11 +18,17 @@ ALU = mybir.AluOpType
 
 P = 128
 PACK = 4
-PASSES = K // (P * PACK)
 N = 512
+PASSES = K // N
 HALVES = S // N
-QUADS = 4
+QUADRANT = 32
+PLANE_ROWS = 4
+LIST_ROWS = 16
 M_TILES = S2 // P
+PAIRS = PACK // 2
+RUN = 4
+
+PIECES = ((0, N), (N, N // 2), (N + N // 2, N // 2))
 
 
 def tile_list_track_blend_rating_kernel(
@@ -32,30 +38,33 @@ def tile_list_track_blend_rating_kernel(
     with ExitStack() as ctx:
         keep = ctx.enter_context(tc.tile_pool(name="keep", bufs=1))
         shared = ctx.enter_context(tc.tile_pool(name="shared", bufs=1))
-        ring = ctx.enter_context(tc.tile_pool(name="ring", bufs=2))
+        ring = ctx.enter_context(tc.tile_pool(name="ring", bufs=3))
         psum = ctx.enter_context(tc.psum_pool(name="psum", bufs=8))
 
         def held(shape, dtype, name):
             return keep.tile(shape, dtype, name=name, align_bytes=64)
 
-        idx = held([P, S // 16], U16, "idx")
-        idx2 = held([P, S2 // 16], U16, "idx2")
-        chunk_bytes = PACK * N * 4
-        small = 64
-        chunk_at = [0, chunk_bytes + small, 2 * chunk_bytes + small, 3 * chunk_bytes + 3 * small]
-
         def placed(shape, dtype, name, offset):
             return shared.tile(shape, dtype, name=name, align_bytes=64, offset=offset)
 
+        def bank(name):
+            return psum.tile([P, N], F32, name=name, tag="bank")
+
+        chunk_bytes = PACK * N * 4
+        slot = 64
+        chunk_at = (0, chunk_bytes + slot, 2 * chunk_bytes + slot, 3 * chunk_bytes + 3 * slot)
+
+        idx = held([P, S // LIST_ROWS], U16, "idx")
+        idx2 = held([P, S2 // LIST_ROWS], U16, "idx2")
         tab_s = placed([P, T], U8, "tab_s", chunk_at[1] - T // 2)
         w4_s_raw = placed([P, PASSES * K], U8, "w4_s_raw", chunk_at[3] - K)
         plane1 = held([P, S + S2], U8, "plane1")
         zero_in = held([P, 1], F32, "zero_in")
         zero = held([P, 1], F32, "zero")
 
-        split = 640
-        nc.gpsimd.memset(tab_s[:].bitcast(I32)[:, :split], 0)
-        nc.vector.memset(tab_s[:].bitcast(I32)[:, split:], 0)
+        gpsimd_words = 640
+        nc.gpsimd.memset(tab_s[:].bitcast(I32)[:, :gpsimd_words], 0)
+        nc.vector.memset(tab_s[:].bitcast(I32)[:, gpsimd_words:], 0)
         nc.vector.memset(w4_s_raw[:].bitcast(I32), 0)
         nc.vector.memset(zero_in[:], 0.0)
         nc.vector.memset(plane1[:].bitcast(I32), 0)
@@ -67,14 +76,17 @@ def tile_list_track_blend_rating_kernel(
         nc.sync.dma_start(w4_raw[:], w4_words.bitcast(I32).rearrange("a p c -> p a c"))
         tab_w = [held([P, T], I32, f"tab_w{a}") for a in range(PASSES)]
         tab_src = [tab_words[a].rearrange("p t i -> p (t i)").bitcast(I32) for a in range(PASSES)]
-        for r in range(4):
-            nc.sync.dma_start(tab_s[r:P:32, :].bitcast(I32), tab_scales[0, r:16:4, :].bitcast(I32))
+        blocks = P // 8
+        for r in range(PLANE_ROWS):
+            nc.sync.dma_start(
+                tab_s[r:P:QUADRANT, :].bitcast(I32), tab_scales[0, r:blocks:PLANE_ROWS, :].bitcast(I32)
+            )
         nc.sync.dma_start(tab_s[4:P:8, :].bitcast(I32), tab_scales[1].bitcast(I32))
         nc.sync.dma_start(tab_w[0][:, : T // 2], tab_src[0][:, : T // 2])
-        for r in range(4):
+        for r in range(PLANE_ROWS):
             nc.sync.dma_start(
-                w4_s_raw[r:P:32, :].bitcast(I32).rearrange("q (a c) -> q a c", a=PASSES),
-                w4_scales[:, r:16:4, :].bitcast(I32).rearrange("a q c -> q a c"),
+                w4_s_raw[r:P:QUADRANT, :].bitcast(I32).rearrange("q (a c) -> q a c", a=PASSES),
+                w4_scales[:, r:blocks:PLANE_ROWS, :].bitcast(I32).rearrange("a q c -> q a c"),
             )
         nc.sync.dma_start(tab_w[0][:, T // 2 :], tab_src[0][:, T // 2 :])
         nc.sync.dma_start(tab_w[1][:], tab_src[1])
@@ -88,237 +100,196 @@ def tile_list_track_blend_rating_kernel(
         plane0 = held([P, S + S2], U8, "plane0")
         nc.vector.tensor_copy(plane0[:, :S], tab_s[:].indirect(idx[:]))
         nc.vector.tensor_copy(plane0[:, S:], tab_s[:].indirect(idx2[:]))
-        for r in range(4):
-            nc.sync.dma_start(plane1[r:P:32, :].bitcast(I32), plane0[4 + 8 * r : P : 32, :].bitcast(I32))
+        for r in range(PLANE_ROWS):
+            nc.sync.dma_start(
+                plane1[r:P:QUADRANT, :].bitcast(I32), plane0[4 + 8 * r : P : QUADRANT, :].bitcast(I32)
+            )
         planes = (plane0, plane1)
         w4_s = held([P, PASSES * K], U8, "w4_s")
         nc.vector.tensor_copy(
             w4_s[:].rearrange("p (g t m) -> p g t m", t=PACK, m=P),
             w4_s_raw[:].rearrange("p (g m t) -> p g t m", t=PACK, m=P),
         )
-        gb_t = placed([P, PASSES, PACK], F32, "gb_t", chunk_at[1] - small)
-        ga_t = placed([P, PASSES, PACK], F32, "ga_t", chunk_at[3] - 2 * small)
-        th_t = placed([P, M_TILES], F32, "th_t", chunk_at[3] - small)
+
+        gb_t = placed([P, PASSES, PACK], F32, "gb_t", chunk_at[1] - slot)
+        ga_t = placed([P, PASSES, PACK], F32, "ga_t", chunk_at[3] - 2 * slot)
+        th_t = placed([P, M_TILES], F32, "th_t", chunk_at[3] - slot)
         neg_th = held([P, M_TILES], F32, "neg_th")
         w1_raw = {}
 
-        def load_w1(rb, a):
-            raw = placed([P, PACK, N], F32, f"w1_raw{rb}{a}", chunk_at[rb * PASSES + a])
+        def load_w1(s, a):
+            raw = placed([P, PACK, N], F32, f"w1_raw{s}{a}", chunk_at[s * PASSES + a])
             nc.sync.dma_start(
-                raw[:],
-                w1[512 * a : 512 * (a + 1), N * rb : N * (rb + 1)].rearrange("(p i) c -> p i c", i=PACK),
+                raw[:], w1[N * a : N * (a + 1), N * s : N * (s + 1)].rearrange("(p i) c -> p i c", i=PACK)
             )
-            w1_raw[rb, a] = raw
+            w1_raw[s, a] = raw
 
-        nc.sync.dma_start(gb_t[:], gb.rearrange("(b p t) -> p b t", b=PASSES, t=PACK))
+        nc.sync.dma_start(gb_t[:], gb.rearrange("(s p t) -> p s t", s=PASSES, t=PACK))
         load_w1(0, 0)
         load_w1(0, 1)
         load_w1(1, 0)
-        nc.sync.dma_start(ga_t[:], ga.rearrange("(b p t) -> p b t", b=PASSES, t=PACK))
+        nc.sync.dma_start(ga_t[:], ga.rearrange("(s p t) -> p s t", s=PASSES, t=PACK))
         load_w1(1, 1)
         with nc.allow_non_contiguous_dma(reason="one threshold a partition"):
             nc.sync.dma_start(th_t[:], th.rearrange("(u p) -> p u", p=P))
+
         v_w = {}
+        for a in range(PASSES):
+            for half in range(HALVES):
+                v_w[a, half] = held([P, N], U32, f"v_w{a}{half}")
+                entries = idx[:, half * N // LIST_ROWS : (half + 1) * N // LIST_ROWS]
+                nc.vector.tensor_copy(v_w[a, half][:], tab_w[a][:].bitcast(U32).indirect(entries))
+
         v2_w = {}
 
-        def gather_v(a):
-            for jh in range(HALVES):
-                words = held([P, N], U32, f"v_w{a}{jh}")
-                cols = slice(jh * N // 16, (jh + 1) * N // 16)
-                nc.vector.tensor_copy(words[:], tab_w[a][:].bitcast(U32).indirect(idx[:, cols]))
-                v_w[a, jh] = words
-
         def gather_v2(a):
-            words = held([P, S2], U32, f"v2_w{a}")
-            nc.vector.tensor_copy(words[:], tab_w[a][:].bitcast(U32).indirect(idx2[:]))
-            v2_w[a] = words
-
-        gather_v(0)
-        gather_v(1)
-
-        def bank(name):
-            return psum.tile([P, N], F32, name=name, tag="bank")
+            v2_w[a] = held([P, S2], U32, f"v2_w{a}")
+            nc.vector.tensor_copy(v2_w[a][:], tab_w[a][:].bitcast(U32).indirect(idx2[:]))
 
         lin = {}
 
-        def l_pass(acc, rb, jh, t, a):
-            c0 = a * K + rb * N + t * P
-            nc.tensor.matmul_mx(
-                out=acc[:],
-                lhsT=w4_w[:, c0 : c0 + P].bitcast(U8).bitcast(FP4X4),
-                lhsT_scale=w4_s[:, c0 : c0 + P],
-                rhs=v_w[a, jh][:].bitcast(FP8X4),
-                rhs_scale=planes[a][:, jh * N : (jh + 1) * N],
-                start=(a == 0),
-                stop=(a == PASSES - 1),
-            )
-
-        def l_out(acc, rb, jh, t):
-            scaled = held([P, N], F32, f"lin{rb}{jh}{t}")
-            nc.scalar.activation(scaled[:], acc[:], ACT.Copy, scale=gb_t[:, rb, t : t + 1])
-            lin[rb, jh, t] = scaled
-
-        def l_groups(groups):
-            tiles = [(rb, jh, t) for rb, jh in groups for t in range(PACK)]
-            accs = {key: bank(f"l{key[0]}{key[1]}{key[2]}") for key in tiles}
+        def linear_part(groups):
+            keys = [(s, half, t) for s, half in groups for t in range(PACK)]
+            sums = {(s, half, t): bank(f"l{s}{half}{t}") for s, half, t in keys}
             for a in range(PASSES):
-                for key in tiles:
-                    l_pass(accs[key], *key, a)
-            for key in tiles:
-                l_out(accs[key], *key)
+                for s, half, t in keys:
+                    cols = slice(a * K + s * N + t * P, a * K + s * N + (t + 1) * P)
+                    nc.tensor.matmul_mx(
+                        out=sums[s, half, t][:],
+                        lhsT=w4_w[:, cols].bitcast(U8).bitcast(FP4X4),
+                        lhsT_scale=w4_s[:, cols],
+                        rhs=v_w[a, half][:].bitcast(FP8X4),
+                        rhs_scale=planes[a][:, half * N : (half + 1) * N],
+                        start=(a == 0),
+                        stop=(a == PASSES - 1),
+                    )
+            for s, half, t in keys:
+                lin[s, half, t] = held([P, N], F32, f"lin{s}{half}{t}")
+                nc.scalar.activation(
+                    lin[s, half, t][:], sums[s, half, t][:], ACT.Copy, scale=gb_t[:, s, t : t + 1]
+                )
 
-        w1_bf = {}
         w1_w = {}
         w1_s = {}
 
-        def w1_cast(rb, a, tp, on_scalar):
-            grouped = held([P, 2, P, PACK], BF16, f"w1_bf{rb}{a}{tp}")
-            src = w1_raw[rb, a][:].rearrange("p i (m t) -> p m i t", t=PACK)[:, :, :, 2 * tp : 2 * tp + 2]
-            dst = grouped[:].rearrange("p t m i -> p m i t")
-            if on_scalar:
-                nc.scalar.copy(dst, src)
-            else:
-                nc.vector.tensor_copy(dst, src)
-            w1_bf[rb, a, tp] = grouped
+        def quantise_w1(s, a):
+            rounded = []
+            for pair in range(PAIRS):
+                grouped = held([P, 2, P, PACK], BF16, f"w1_bf{s}{a}{pair}")
+                by_channel = w1_raw[s, a][:].rearrange("p i (m t) -> p m i t", t=PACK)
+                nc.vector.tensor_copy(
+                    grouped[:].rearrange("p t m i -> p m i t"), by_channel[:, :, :, 2 * pair : 2 * pair + 2]
+                )
+                rounded.append(grouped)
+            for pair in range(PAIRS):
+                w1_w[s, a, pair] = held([P, 2 * P], U32, f"w1_w{s}{a}{pair}")
+                w1_s[s, a, pair] = held([P, 2 * P], U8, f"w1_s{s}{a}{pair}")
+                nc.vector.quantize_mx(
+                    out=w1_w[s, a, pair][:].bitcast(FP8X4),
+                    scales=w1_s[s, a, pair][:],
+                    in_=rounded[pair][:].rearrange("p t m i -> p (t m i)"),
+                )
 
-        def w1_quant(rb, a, tp):
-            codes = held([P, 2 * P], U32, f"w1_w{rb}{a}{tp}")
-            scales = held([P, 2 * P], U8, f"w1_s{rb}{a}{tp}")
-            nc.vector.quantize_mx(
-                out=codes[:].bitcast(FP8X4),
-                scales=scales[:],
-                in_=w1_bf[rb, a, tp][:].rearrange("p t m i -> p (t m i)"),
-            )
-            w1_w[rb, a, tp] = codes
-            w1_s[rb, a, tp] = scales
+        bounded = {}
 
-        def w1_chunk(rb, a, scalar_pairs):
-            for tp in range(2):
-                w1_cast(rb, a, tp, tp in scalar_pairs)
-            for tp in range(2):
-                w1_quant(rb, a, tp)
+        def bounded_part(s, half):
+            for t in range(PACK):
+                acc = bank(f"b{s}{half}{t}")
+                cols = slice((t % 2) * P, (t % 2 + 1) * P)
+                for a in range(PASSES):
+                    nc.tensor.matmul_mx(
+                        out=acc[:],
+                        lhsT=w1_w[s, a, t // 2][:, cols].bitcast(FP8X4),
+                        lhsT_scale=w1_s[s, a, t // 2][:, cols],
+                        rhs=v_w[a, half][:].bitcast(FP8X4),
+                        rhs_scale=planes[a][:, half * N : (half + 1) * N],
+                        start=(a == 0),
+                        stop=(a == PASSES - 1),
+                    )
+                bounded[s, half, t] = ring.tile([P, N], F32, name="bounded", bufs=3 * PACK, align_bytes=64)
+                nc.scalar.activation(bounded[s, half, t][:], acc[:], ACT.Tanh, bias=zero[:])
 
+        rows = {}
+        woven = {}
         h_w = {}
         h_s = {}
-        bounded = {}
-        rows = {}
 
-        def b_tile(rb, j0, width, t):
-            jh, c0 = divmod(j0, N)
-            acc = bank(f"b{rb}{j0}{t}")
-            cols = slice((t % 2) * P, (t % 2 + 1) * P)
-            for a in range(PASSES):
-                nc.tensor.matmul_mx(
-                    out=acc[:, :width],
-                    lhsT=w1_w[rb, a, t // 2][:, cols].bitcast(FP8X4),
-                    lhsT_scale=w1_s[rb, a, t // 2][:, cols],
-                    rhs=v_w[a, jh][:, c0 : c0 + width].bitcast(FP8X4),
-                    rhs_scale=planes[a][:, j0 : j0 + width],
-                    start=(a == 0),
-                    stop=(a == PASSES - 1),
+        def blend(s, j0, width):
+            half, c0 = divmod(j0, N)
+            rows[s, j0] = ring.tile([P, PACK, width], BF16, name="h_rows", align_bytes=64)
+            for t in range(PACK):
+                nc.vector.scalar_tensor_tensor(
+                    out=rows[s, j0][:, t, :],
+                    in0=bounded[s, half, t][:, c0 : c0 + width],
+                    scalar=ga_t[:, s, t : t + 1],
+                    in1=lin[s, half, t][:, c0 : c0 + width],
+                    op0=ALU.mult,
+                    op1=ALU.add,
                 )
-            values = ring.tile([P, width], F32, name="bounded", bufs=8, align_bytes=64)
-            nc.scalar.activation(values[:], acc[:, :width], ACT.Tanh, bias=zero[:])
-            bounded[rb, j0, t] = values
 
-        def h_row(rb, j0, width, t):
-            jh, c0 = divmod(j0, N)
-            if t == 0:
-                rows[rb, j0] = ring.tile([P, PACK, width], BF16, name="h_rows", bufs=3, align_bytes=64)
-            nc.vector.scalar_tensor_tensor(
-                out=rows[rb, j0][:, t, :],
-                in0=bounded[rb, j0, t][:],
-                scalar=ga_t[:, rb, t : t + 1],
-                in1=lin[rb, jh, t][:, c0 : c0 + width],
-                op0=ALU.mult,
-                op1=ALU.add,
-            )
-
-        woven = {}
-
-        def h_weave(rb, j0, width, copy=nc.vector.tensor_copy):
-            woven[rb, j0] = ring.tile([P, width, PACK], BF16, name="h_woven", bufs=3, align_bytes=64)
+        def weave(s, j0, width, copy):
+            woven[s, j0] = ring.tile([P, width, PACK], BF16, name="h_woven", align_bytes=64)
             copy(
-                woven[rb, j0][:].rearrange("p (c i) t -> p c t i", i=4),
-                rows[rb, j0][:].rearrange("p t (c i) -> p c t i", i=4),
+                woven[s, j0][:].rearrange("p (c i) t -> p c t i", i=RUN),
+                rows[s, j0][:].rearrange("p t (c i) -> p c t i", i=RUN),
             )
 
-        def h_quant(rb, j0, width):
-            codes = held([P, width], U32, f"h_w{rb}{j0}")
-            scales = held([P, width], U8, f"h_s{rb}{j0}")
+        def quantise_h(s, j0, width):
+            h_w[s, j0] = held([P, width], U32, f"h_w{s}{j0}")
+            h_s[s, j0] = held([P, width], U8, f"h_s{s}{j0}")
             nc.vector.quantize_mx(
-                out=codes[:].bitcast(FP8X4), scales=scales[:], in_=woven[rb, j0][:].rearrange("p n t -> p (n t)")
+                out=h_w[s, j0][:].bitcast(FP8X4),
+                scales=h_s[s, j0][:],
+                in_=woven[s, j0][:].rearrange("p n t -> p (n t)"),
             )
-            h_w[rb, j0] = codes
-            h_s[rb, j0] = scales
-
-        def h_cols(pieces, rb, j0, width):
-            start = max(s for r, s in pieces if r == rb and s <= j0)
-            return pieces[rb, start][:, j0 - start : j0 - start + width]
-
-        def negate_th():
-            nc.scalar.mul(neg_th[:], th_t[:], -1.0)
 
         def rate(j0, width):
             for u in range(M_TILES):
                 acc = bank(f"e{j0}{u}")
-                cols = slice(u * P, (u + 1) * P)
-                for rb in range(PASSES):
+                for s in range(PASSES):
                     nc.tensor.matmul_mx(
                         out=acc[:, :width],
-                        lhsT=v2_w[rb][:, cols].bitcast(FP8X4),
-                        lhsT_scale=planes[rb][:, S + u * P : S + (u + 1) * P],
-                        rhs=h_cols(h_w, rb, j0, width).bitcast(FP8X4),
-                        rhs_scale=h_cols(h_s, rb, j0, width),
-                        start=(rb == 0),
-                        stop=(rb == PASSES - 1),
+                        lhsT=v2_w[s][:, u * P : (u + 1) * P].bitcast(FP8X4),
+                        lhsT_scale=planes[s][:, S + u * P : S + (u + 1) * P],
+                        rhs=h_w[s, j0][:].bitcast(FP8X4),
+                        rhs_scale=h_s[s, j0][:],
+                        start=(s == 0),
+                        stop=(s == PASSES - 1),
                     )
-                result = ring.tile([P, width], F32, name="result", bufs=12, align_bytes=64)
+                result = ring.tile([P, width], F32, name="result", bufs=len(PIECES) * M_TILES, align_bytes=64)
                 nc.scalar.activation(result[:], acc[:, :width], ACT.Silu, bias=neg_th[:, u : u + 1])
                 nc.sync.dma_start(out[u * P : (u + 1) * P, j0 : j0 + width], result[:])
 
-        def b_group(rb, j0, width):
-            for t in range(PACK):
-                b_tile(rb, j0, width, t)
+        def finish(s, j0, width):
+            quantise_h(s, j0, width)
+            if s == PASSES - 1:
+                rate(j0, width)
 
-        def h_rows(rb, j0, width):
-            for t in range(PACK):
-                h_row(rb, j0, width, t)
-
-        l_groups([(0, 0), (1, 0)])
+        linear_part([(0, 0), (1, 0)])
         gather_v2(0)
         gather_v2(1)
-        w1_chunk(0, 0, ())
-        l_groups([(0, 1)])
-        w1_chunk(0, 1, ())
-        b_group(0, 0, N)
-        w1_chunk(1, 0, ())
-        l_groups([(1, 1)])
-        w1_chunk(1, 1, ())
-        negate_th()
-        b_group(1, 0, 512)
-        b_group(0, 512, 256)
-        h_rows(0, 0, 512)
-        b_group(1, 512, 256)
-        h_weave(0, 0, 512, nc.scalar.copy)
-        h_rows(1, 0, 512)
-        b_group(0, 768, 256)
-        h_quant(0, 0, 512)
-        h_weave(1, 0, 512)
-        h_rows(0, 512, 256)
-        b_group(1, 768, 256)
-        h_quant(1, 0, 512)
-        rate(0, 512)
-        h_weave(0, 512, 256)
-        h_rows(1, 512, 256)
-        h_quant(0, 512, 256)
-        h_weave(1, 512, 256)
-        h_rows(0, 768, 256)
-        h_weave(0, 768, 256, nc.scalar.copy)
-        h_quant(1, 512, 256)
-        rate(512, 256)
-        h_rows(1, 768, 256)
-        h_quant(0, 768, 256)
-        h_weave(1, 768, 256)
-        h_quant(1, 768, 256)
-        rate(768, 256)
+        quantise_w1(0, 0)
+        linear_part([(0, 1)])
+        quantise_w1(0, 1)
+        bounded_part(0, 0)
+        quantise_w1(1, 0)
+        linear_part([(1, 1)])
+        quantise_w1(1, 1)
+        nc.scalar.mul(neg_th[:], th_t[:], -1.0)
+        bounded_part(1, 0)
+        bounded_part(0, 1)
+
+        units = [(s, j0, width) for j0, width in PIECES for s in range(PASSES)]
+        last_of_first_half = PASSES - 1
+        woven_by_scalar = len(units) - PASSES
+        for k, unit in enumerate(units):
+            blend(*unit)
+            if k == last_of_first_half:
+                bounded_part(1, 1)
+            if k == woven_by_scalar:
+                weave(*unit, nc.scalar.copy)
+            if k > 0:
+                finish(*units[k - 1])
+            if k != woven_by_scalar:
+                weave(*unit, nc.vector.tensor_copy)
+        finish(*units[-1])

from contextlib import ExitStack

import concourse.mybir as mybir

K, T, S, S2 = 1024, 4096, 1024, 512
FLOPS = 2 * K * K * S * 2 + 2 * K * S2 * S

F32 = mybir.dt.float32
BF16 = mybir.dt.bfloat16
I32 = mybir.dt.int32
U32 = mybir.dt.uint32
U16 = mybir.dt.uint16
U8 = mybir.dt.uint8
FP8X4 = mybir.dt.float8_e4m3fn_x4
FP4X4 = mybir.dt.float4_e2m1fn_x4
ACT = mybir.ActivationFunctionType
ALU = mybir.AluOpType

P = 128
PACK = 4
N = 512
PASSES = K // N
HALVES = S // N
QUADRANT = 32
PLANE_ROWS = 4
LIST_ROWS = 16
M_TILES = S2 // P
PAIRS = PACK // 2
RUN = 4

PIECES = ((0, N), (N, N // 2), (N + N // 2, N // 2))


def tile_list_track_blend_rating_kernel(
    tc, tab_words, tab_scales, offs, offs2, w1, w4_words, w4_scales, ga, gb, th, out
):
    nc = tc.nc
    with ExitStack() as ctx:
        keep = ctx.enter_context(tc.tile_pool(name="keep", bufs=1))
        shared = ctx.enter_context(tc.tile_pool(name="shared", bufs=1))
        ring = ctx.enter_context(tc.tile_pool(name="ring", bufs=3))
        psum = ctx.enter_context(tc.psum_pool(name="psum", bufs=8))

        def held(shape, dtype, name):
            return keep.tile(shape, dtype, name=name, align_bytes=64)

        def placed(shape, dtype, name, offset):
            return shared.tile(shape, dtype, name=name, align_bytes=64, offset=offset)

        def bank(name):
            return psum.tile([P, N], F32, name=name, tag="bank")

        chunk_bytes = PACK * N * 4
        slot = 64
        chunk_at = (0, chunk_bytes + slot, 2 * chunk_bytes + slot, 3 * chunk_bytes + 3 * slot)

        idx = held([P, S // LIST_ROWS], U16, "idx")
        idx2 = held([P, S2 // LIST_ROWS], U16, "idx2")
        tab_s = placed([P, T], U8, "tab_s", chunk_at[1] - T // 2)
        w4_s_raw = placed([P, PASSES * K], U8, "w4_s_raw", chunk_at[3] - K)
        plane1 = held([P, S + S2], U8, "plane1")
        zero_in = held([P, 1], F32, "zero_in")
        zero = held([P, 1], F32, "zero")

        gpsimd_words = 640
        nc.gpsimd.memset(tab_s[:].bitcast(I32)[:, :gpsimd_words], 0)
        nc.vector.memset(tab_s[:].bitcast(I32)[:, gpsimd_words:], 0)
        nc.vector.memset(w4_s_raw[:].bitcast(I32), 0)
        nc.vector.memset(zero_in[:], 0.0)
        nc.vector.memset(plane1[:].bitcast(I32), 0)
        nc.scalar.activation(zero[:], zero_in[:], ACT.Silu)

        nc.sync.dma_start(idx[:], offs)
        nc.sync.dma_start(idx2[:], offs2)
        w4_raw = held([P, PASSES, K // 2], I32, "w4_raw")
        nc.sync.dma_start(w4_raw[:], w4_words.bitcast(I32).rearrange("a p c -> p a c"))
        tab_w = [held([P, T], I32, f"tab_w{a}") for a in range(PASSES)]
        tab_src = [tab_words[a].rearrange("p t i -> p (t i)").bitcast(I32) for a in range(PASSES)]
        blocks = P // 8
        for r in range(PLANE_ROWS):
            nc.sync.dma_start(
                tab_s[r:P:QUADRANT, :].bitcast(I32), tab_scales[0, r:blocks:PLANE_ROWS, :].bitcast(I32)
            )
        nc.sync.dma_start(tab_s[4:P:8, :].bitcast(I32), tab_scales[1].bitcast(I32))
        nc.sync.dma_start(tab_w[0][:, : T // 2], tab_src[0][:, : T // 2])
        for r in range(PLANE_ROWS):
            nc.sync.dma_start(
                w4_s_raw[r:P:QUADRANT, :].bitcast(I32).rearrange("q (a c) -> q a c", a=PASSES),
                w4_scales[:, r:blocks:PLANE_ROWS, :].bitcast(I32).rearrange("a q c -> q a c"),
            )
        nc.sync.dma_start(tab_w[0][:, T // 2 :], tab_src[0][:, T // 2 :])
        nc.sync.dma_start(tab_w[1][:], tab_src[1])

        w4_w = held([P, PASSES * K], U16, "w4_w")
        nc.vector.tensor_copy(
            w4_w[:].rearrange("p (g t m) -> p g t m", t=PACK, m=P),
            w4_raw[:].rearrange("p a c -> p (a c)").bitcast(U16).rearrange("p (g m t) -> p g t m", t=PACK, m=P),
        )

        plane0 = held([P, S + S2], U8, "plane0")
        nc.vector.tensor_copy(plane0[:, :S], tab_s[:].indirect(idx[:]))
        nc.vector.tensor_copy(plane0[:, S:], tab_s[:].indirect(idx2[:]))
        for r in range(PLANE_ROWS):
            nc.sync.dma_start(
                plane1[r:P:QUADRANT, :].bitcast(I32), plane0[4 + 8 * r : P : QUADRANT, :].bitcast(I32)
            )
        planes = (plane0, plane1)
        w4_s = held([P, PASSES * K], U8, "w4_s")
        nc.vector.tensor_copy(
            w4_s[:].rearrange("p (g t m) -> p g t m", t=PACK, m=P),
            w4_s_raw[:].rearrange("p (g m t) -> p g t m", t=PACK, m=P),
        )

        gb_t = placed([P, PASSES, PACK], F32, "gb_t", chunk_at[1] - slot)
        ga_t = placed([P, PASSES, PACK], F32, "ga_t", chunk_at[3] - 2 * slot)
        th_t = placed([P, M_TILES], F32, "th_t", chunk_at[3] - slot)
        neg_th = held([P, M_TILES], F32, "neg_th")
        w1_raw = {}

        def load_w1(s, a):
            raw = placed([P, PACK, N], F32, f"w1_raw{s}{a}", chunk_at[s * PASSES + a])
            nc.sync.dma_start(
                raw[:], w1[N * a : N * (a + 1), N * s : N * (s + 1)].rearrange("(p i) c -> p i c", i=PACK)
            )
            w1_raw[s, a] = raw

        nc.sync.dma_start(gb_t[:], gb.rearrange("(s p t) -> p s t", s=PASSES, t=PACK))
        load_w1(0, 0)
        load_w1(0, 1)
        load_w1(1, 0)
        nc.sync.dma_start(ga_t[:], ga.rearrange("(s p t) -> p s t", s=PASSES, t=PACK))
        load_w1(1, 1)
        with nc.allow_non_contiguous_dma(reason="one threshold a partition"):
            nc.sync.dma_start(th_t[:], th.rearrange("(u p) -> p u", p=P))

        v_w = {}
        for a in range(PASSES):
            for half in range(HALVES):
                v_w[a, half] = held([P, N], U32, f"v_w{a}{half}")
                entries = idx[:, half * N // LIST_ROWS : (half + 1) * N // LIST_ROWS]
                nc.vector.tensor_copy(v_w[a, half][:], tab_w[a][:].bitcast(U32).indirect(entries))

        v2_w = {}

        def gather_v2(a):
            v2_w[a] = held([P, S2], U32, f"v2_w{a}")
            nc.vector.tensor_copy(v2_w[a][:], tab_w[a][:].bitcast(U32).indirect(idx2[:]))

        lin = {}

        def linear_part(groups):
            keys = [(s, half, t) for s, half in groups for t in range(PACK)]
            sums = {(s, half, t): bank(f"l{s}{half}{t}") for s, half, t in keys}
            for a in range(PASSES):
                for s, half, t in keys:
                    cols = slice(a * K + s * N + t * P, a * K + s * N + (t + 1) * P)
                    nc.tensor.matmul_mx(
                        out=sums[s, half, t][:],
                        lhsT=w4_w[:, cols].bitcast(U8).bitcast(FP4X4),
                        lhsT_scale=w4_s[:, cols],
                        rhs=v_w[a, half][:].bitcast(FP8X4),
                        rhs_scale=planes[a][:, half * N : (half + 1) * N],
                        start=(a == 0),
                        stop=(a == PASSES - 1),
                    )
            for s, half, t in keys:
                lin[s, half, t] = held([P, N], F32, f"lin{s}{half}{t}")
                nc.scalar.activation(
                    lin[s, half, t][:], sums[s, half, t][:], ACT.Copy, scale=gb_t[:, s, t : t + 1]
                )

        w1_w = {}
        w1_s = {}

        def quantise_w1(s, a):
            rounded = []
            for pair in range(PAIRS):
                grouped = held([P, 2, P, PACK], BF16, f"w1_bf{s}{a}{pair}")
                by_channel = w1_raw[s, a][:].rearrange("p i (m t) -> p m i t", t=PACK)
                nc.vector.tensor_copy(
                    grouped[:].rearrange("p t m i -> p m i t"), by_channel[:, :, :, 2 * pair : 2 * pair + 2]
                )
                rounded.append(grouped)
            for pair in range(PAIRS):
                w1_w[s, a, pair] = held([P, 2 * P], U32, f"w1_w{s}{a}{pair}")
                w1_s[s, a, pair] = held([P, 2 * P], U8, f"w1_s{s}{a}{pair}")
                nc.vector.quantize_mx(
                    out=w1_w[s, a, pair][:].bitcast(FP8X4),
                    scales=w1_s[s, a, pair][:],
                    in_=rounded[pair][:].rearrange("p t m i -> p (t m i)"),
                )

        bounded = {}

        def bounded_part(s, half):
            for t in range(PACK):
                acc = bank(f"b{s}{half}{t}")
                cols = slice((t % 2) * P, (t % 2 + 1) * P)
                for a in range(PASSES):
                    nc.tensor.matmul_mx(
                        out=acc[:],
                        lhsT=w1_w[s, a, t // 2][:, cols].bitcast(FP8X4),
                        lhsT_scale=w1_s[s, a, t // 2][:, cols],
                        rhs=v_w[a, half][:].bitcast(FP8X4),
                        rhs_scale=planes[a][:, half * N : (half + 1) * N],
                        start=(a == 0),
                        stop=(a == PASSES - 1),
                    )
                bounded[s, half, t] = ring.tile([P, N], F32, name="bounded", bufs=3 * PACK, align_bytes=64)
                nc.scalar.activation(bounded[s, half, t][:], acc[:], ACT.Tanh, bias=zero[:])

        rows = {}
        woven = {}
        h_w = {}
        h_s = {}

        def blend(s, j0, width):
            half, c0 = divmod(j0, N)
            rows[s, j0] = ring.tile([P, PACK, width], BF16, name="h_rows", align_bytes=64)
            for t in range(PACK):
                nc.vector.scalar_tensor_tensor(
                    out=rows[s, j0][:, t, :],
                    in0=bounded[s, half, t][:, c0 : c0 + width],
                    scalar=ga_t[:, s, t : t + 1],
                    in1=lin[s, half, t][:, c0 : c0 + width],
                    op0=ALU.mult,
                    op1=ALU.add,
                )

        def weave(s, j0, width, copy):
            woven[s, j0] = ring.tile([P, width, PACK], BF16, name="h_woven", align_bytes=64)
            copy(
                woven[s, j0][:].rearrange("p (c i) t -> p c t i", i=RUN),
                rows[s, j0][:].rearrange("p t (c i) -> p c t i", i=RUN),
            )

        def quantise_h(s, j0, width):
            h_w[s, j0] = held([P, width], U32, f"h_w{s}{j0}")
            h_s[s, j0] = held([P, width], U8, f"h_s{s}{j0}")
            nc.vector.quantize_mx(
                out=h_w[s, j0][:].bitcast(FP8X4),
                scales=h_s[s, j0][:],
                in_=woven[s, j0][:].rearrange("p n t -> p (n t)"),
            )

        def rate(j0, width):
            for u in range(M_TILES):
                acc = bank(f"e{j0}{u}")
                for s in range(PASSES):
                    nc.tensor.matmul_mx(
                        out=acc[:, :width],
                        lhsT=v2_w[s][:, u * P : (u + 1) * P].bitcast(FP8X4),
                        lhsT_scale=planes[s][:, S + u * P : S + (u + 1) * P],
                        rhs=h_w[s, j0][:].bitcast(FP8X4),
                        rhs_scale=h_s[s, j0][:],
                        start=(s == 0),
                        stop=(s == PASSES - 1),
                    )
                result = ring.tile([P, width], F32, name="result", bufs=len(PIECES) * M_TILES, align_bytes=64)
                nc.scalar.activation(result[:], acc[:, :width], ACT.Silu, bias=neg_th[:, u : u + 1])
                nc.sync.dma_start(out[u * P : (u + 1) * P, j0 : j0 + width], result[:])

        def finish(s, j0, width):
            quantise_h(s, j0, width)
            if s == PASSES - 1:
                rate(j0, width)

        linear_part([(0, 0), (1, 0)])
        gather_v2(0)
        gather_v2(1)
        quantise_w1(0, 0)
        linear_part([(0, 1)])
        quantise_w1(0, 1)
        bounded_part(0, 0)
        quantise_w1(1, 0)
        linear_part([(1, 1)])
        quantise_w1(1, 1)
        nc.scalar.mul(neg_th[:], th_t[:], -1.0)
        bounded_part(1, 0)
        bounded_part(0, 1)

        units = [(s, j0, width) for j0, width in PIECES for s in range(PASSES)]
        last_of_first_half = PASSES - 1
        woven_by_scalar = len(units) - PASSES
        for k, unit in enumerate(units):
            blend(*unit)
            if k == last_of_first_half:
                bounded_part(1, 1)
            if k == woven_by_scalar:
                weave(*unit, nc.scalar.copy)
            if k > 0:
                finish(*units[k - 1])
            if k != woven_by_scalar:
                weave(*unit, nc.vector.tensor_copy)
        finish(*units[-1])
